import numpy as np
import ml_dtypes


def mxq(x, axis, fmt="e4m3"):
    dtype, down = {"e4m3": (ml_dtypes.float8_e4m3fn, 7), "e5m2": (ml_dtypes.float8_e5m2, 14)}[fmt]
    v = np.moveaxis(np.asarray(x, np.float32).astype(ml_dtypes.bfloat16).astype(np.float64), axis, -1)
    blocks = v.reshape(v.shape[:-1] + (-1, 32))
    amax = np.abs(blocks).max(-1, keepdims=True)
    byte = np.maximum(np.where(amax > 0, np.frexp(amax)[1] - 1 + 127, 0) - down, 1)
    scale = np.exp2(byte - 127.0)
    codes = (blocks / scale).astype(np.float32).astype(dtype).astype(np.float64)
    return np.moveaxis((codes * scale).reshape(v.shape), -1, axis)


WIDE = False


def mx_kscale(k):
    if not WIDE:
        return np.ones(k)
    levels = np.array([10, -10, 5, -5, 0])
    if k % 512:
        return np.exp2(np.random.permutation(np.resize(levels, k // 32))).repeat(32)
    a = np.empty((k // 512, 16))
    for p in range(k // 512):
        a[p, :8] = np.random.permutation(np.resize(levels, 8))
        for g in range(8):
            far = levels[np.abs(levels - a[p, g]) >= 10]
            a[p, g + 8] = far[np.random.randint(len(far))]
    return np.exp2(a.ravel()).repeat(32)


def f64(x):
    return np.asarray(x).astype(np.float64)


def striped(idx):
    return np.tile(np.asarray(idx).reshape(-1, 16).T, (8, 1)).astype(np.uint16)


def unstriped(offs):
    return offs[:16].T.reshape(-1).astype(np.int64)


E2M1 = np.array([0.0, 0.5, 1.0, 1.5, 2.0, 3.0, 4.0, 6.0, -0.0, -0.5, -1.0, -1.5, -2.0, -3.0, -4.0, -6.0])


def pack_weight(w, fmt):
    k, n = w.shape
    w = f64(np.asarray(w, np.float32).astype(ml_dtypes.bfloat16)).reshape(k // 32, 32, n)
    amax = np.abs(w).max(1)
    if fmt == "e4m3":
        byte = np.frexp(amax)[1] - 1 + 127 - 7
    else:
        mant, ex = np.frexp(amax / 6.0)
        byte = np.where(mant > 0.5, ex, ex - 1) + 127
    byte = np.clip(np.where(amax > 0, byte, 1), 1, 254)
    scaled = (w * np.exp2(127.0 - byte)[:, None, :]).reshape(k, n).astype(np.float32)
    by_word = np.ascontiguousarray(scaled.reshape(k // 512, 128, 4, n).transpose(0, 1, 3, 2))
    if fmt == "e4m3":
        words = by_word.astype(ml_dtypes.float8_e4m3fn).view(np.uint8)
    else:
        c = by_word.astype(ml_dtypes.float4_e2m1fn).view(np.uint8) & 0xF
        words = (c[..., 0::2] | (c[..., 1::2] << 4)).reshape(k // 512, 128, 2 * n)
    return np.ascontiguousarray(words), np.ascontiguousarray(byte.astype(np.uint8).reshape(k // 512, 16, n))


def unpack_weight(words, scales, fmt):
    g, _, n = scales.shape
    words = np.ascontiguousarray(words).reshape(g, 128, n, -1)
    if fmt == "e4m3":
        vals = words.view(ml_dtypes.float8_e4m3fn).astype(np.float64)
    else:
        nib = np.empty((g, 128, n, 4), np.uint8)
        nib[..., 0::2] = words & 0xF
        nib[..., 1::2] = words >> 4
        vals = E2M1[nib]
    vals = vals * np.repeat(np.exp2(scales.astype(np.float64) - 127.0), 8, axis=1)[..., None]
    return vals.transpose(0, 1, 3, 2).reshape(g * 512, n)


K, R, F, T, J, G = 512, 128, 512, 2048, 512, 32


def setup_inputs():
    n = np.random.standard_normal
    idx = np.random.permutation(T)[:J]
    fk = mx_kscale(K)
    ff = mx_kscale(F)
    tabp = pack_weight(n((K, T)) / fk[:, None], "e4m3")
    return {
        "tab_words": tabp[0],
        "tab_scales": tabp[1],
        "w1": (n((K, R)) * 1 / np.sqrt(K) * fk[:, None]).astype(np.float32),
        "sharp": (np.random.uniform(0.3, 1.5, (R, 1))).astype(np.float32),
        "wo": (n((F, R)) * 1 / np.sqrt(F) * ff[:, None]).astype(np.float32),
        "dy": (n((F, J)) / ff[:, None]).astype(np.float32),
        "old": (0.5 * n((R, J))).astype(np.float32),
        "offs": striped(idx),
    }


def reference(tab_words, tab_scales, w1, sharp, wo, dy, old, offs):
    idx = unstriped(offs)
    tabu = unpack_weight(tab_words, tab_scales, "e4m3")
    w1q = mxq(f64(w1), 0, "e4m3")
    tabidxg = tabu[:, idx]
    a = w1q.T @ tabidxg
    m1 = a.reshape(R, G, J // G).mean(axis=2)
    mr = np.repeat(m1, J // G, axis=1)
    ce = a - mr
    woq = mxq(f64(wo), 0, "e4m3")
    dyq = mxq(f64(dy), 0, "e4m3")
    c0 = woq.T @ dyq
    dce = c0 * a / np.square(np.square(ce) * f64(sharp) + 1.0) * (-1.0) * f64(sharp) * ce * 2.0
    dmr = dce * (-1.0)
    dm1 = dmr.reshape(R, G, J // G).sum(axis=2)
    e1 = dm1 / 16.0
    r1 = np.repeat(e1, J // G, axis=1)
    da = c0 / (np.square(ce) * f64(sharp) + 1.0) + dce + r1
    y = da + f64(old)
    return y

@@ -1,0 +1,185 @@
+from contextlib import ExitStack
+
+import concourse.mybir as mybir
+
+F32 = mybir.dt.float32
+BF16 = mybir.dt.bfloat16
+I32 = mybir.dt.int32
+U32 = mybir.dt.uint32
+U16 = mybir.dt.uint16
+U8 = mybir.dt.uint8
+FP8X4 = mybir.dt.float8_e4m3fn_x4
+ALU = mybir.AluOpType
+ACT = mybir.ActivationFunctionType
+AX = mybir.AxisListType
+
+P = 128
+PACK = 4
+K, R, F, T, J, GROUP = 512, 128, 512, 2048, 512, 16
+HALF = J // 2
+FLOPS = 2 * K * R * J + 2 * F * R * J
+
+
+def interleave(copy, grouped, raw):
+    copy(
+        out=grouped.rearrange("p (c i) t -> p c t i", i=4),
+        in_=raw.rearrange("p t (c i) -> p c t i", i=4),
+    )
+
+
+def by_group(ap):
+    return ap.rearrange("p (g i) -> p g i", i=GROUP)
+
+
+def tile_attend_ccontrastpool_kernel(tc, tab_words, tab_scales, w1, sharp, wo, dy, old, offs, out):
+    nc = tc.nc
+    halves = range(2)
+    with ExitStack() as ctx:
+        sb = ctx.enter_context(tc.tile_pool(name="sb", bufs=1))
+        ps = ctx.enter_context(tc.psum_pool(name="ps", bufs=1))
+
+        def tile(name, shape, dtype):
+            return sb.tile(shape, dtype, name=name, align_bytes=64)
+
+        offsets = sb.tile([P, J // 16], U16, name="offsets")
+        scale_win = tile("scale_win", [P, T], U8)
+        word_win = tile("word_win", [P, T], U32)
+        w1_raw = tile("w1_raw", [P, PACK, R], F32)
+        wo_raw = tile("wo_raw", [P, PACK, R], F32)
+        dy_raw = [tile("dy_raw%d" % h, [P, PACK, HALF], F32) for h in halves]
+        old_sb = tile("old_sb", [P, J], F32)
+        sharp_sb = tile("sharp_sb", [P, 1], F32)
+        warm_out = tile("warm_out", [P, 1], F32)
+
+        nc.vector.memset(scale_win[:, : T // 2].bitcast(I32), 0)
+        nc.gpsimd.memset(scale_win[:, T // 2 :].bitcast(I32), 0)
+        nc.sync.dma_start(offsets[:], offs)
+        nc.sync.dma_start(out=sharp_sb[:], in_=sharp)
+        nc.sync.dma_start(out=w1_raw[:], in_=w1.rearrange("(p t) r -> p t r", t=PACK))
+        for q in range(4):
+            nc.sync.dma_start(
+                out=scale_win[32 * q : 32 * q + 4, :].bitcast(I32),
+                in_=tab_scales[0, 4 * q : 4 * q + 4, :].bitcast(I32),
+            )
+        nc.scalar.activation(out=warm_out[:], in_=sharp_sb[:], func=ACT.Abs_reciprocal_sqrt)
+        nc.sync.dma_start(
+            out=word_win[:].bitcast(I32),
+            in_=tab_words[0].rearrange("p n t -> p (n t)").bitcast(I32),
+        )
+        nc.sync.dma_start(out=wo_raw[:], in_=wo.rearrange("(p t) r -> p t r", t=PACK))
+        dy_rows = dy.rearrange("(p t) j -> p t j", t=PACK)
+        for h in halves:
+            nc.sync.dma_start(out=dy_raw[h][:], in_=dy_rows[:, :, h * HALF : (h + 1) * HALF])
+        nc.sync.dma_start(out=old_sb[:], in_=old)
+
+        def quantise(name, grouped, width):
+            codes = tile(name + "_codes", [P, width], U32)
+            scales = tile(name + "_scales", [P, width], U8)
+            nc.vector.quantize_mx(
+                out=codes[:].bitcast(FP8X4),
+                scales=scales[:],
+                in_=grouped[:].rearrange("p c t -> p (c t)"),
+            )
+            return codes, scales
+
+        w1_grouped = tile("w1_grouped", [P, R, PACK], BF16)
+        interleave(nc.vector.tensor_copy, w1_grouped[:], w1_raw[:])
+        tab_scale = tile("tab_scale", [P, J], U8)
+        nc.vector.tensor_copy(tab_scale[:], scale_win[:].indirect(offsets[:]))
+        w1_codes, w1_scales = quantise("w1", w1_grouped, R)
+
+        slope = tile("slope", [P, 1], F32)
+        nc.vector.tensor_scalar(slope[:], sharp_sb[:], -2.0, None, ALU.mult)
+
+        a = [ps.tile([P, HALF], F32, name="a%d" % h) for h in halves]
+        c0 = [ps.tile([P, HALF], F32, name="c%d" % h) for h in halves]
+        for h in halves:
+            tab_code = tile("tab_code%d" % h, [P, HALF], U32)
+            cols = slice(h * HALF // 16, (h + 1) * HALF // 16)
+            nc.vector.tensor_copy(tab_code[:], word_win[:].indirect(offsets[:, cols]))
+            nc.tensor.matmul_mx(
+                out=a[h][:],
+                lhsT=w1_codes[:].bitcast(FP8X4),
+                lhsT_scale=w1_scales[:],
+                rhs=tab_code[:].bitcast(FP8X4),
+                rhs_scale=tab_scale[:, h * HALF : (h + 1) * HALF],
+                start=True,
+                stop=True,
+            )
+
+        wo_grouped = tile("wo_grouped", [P, R, PACK], BF16)
+        interleave(nc.scalar.copy, wo_grouped[:], wo_raw[:])
+        dy_grouped = [tile("dy_grouped%d" % h, [P, HALF, PACK], BF16) for h in halves]
+        interleave(nc.scalar.copy, dy_grouped[0][:], dy_raw[0][:])
+        wo_codes, wo_scales = quantise("wo", wo_grouped, R)
+
+        def work(name):
+            return [tile("%s%d" % (name, h), [P, HALF], F32) for h in halves]
+
+        def sums(name):
+            return [tile("%s%d" % (name, h), [P, HALF // GROUP], F32) for h in halves]
+
+        def spread(t):
+            return t[:].unsqueeze(2).to_broadcast([P, HALF // GROUP, GROUP])
+
+        a_sum = sums("a_sum")
+        ce = work("ce")
+        for h in halves:
+            nc.vector.tensor_reduce(a_sum[h][:], by_group(a[h][:]), AX.X, ALU.add)
+        for h in halves:
+            nc.vector.scalar_tensor_tensor(
+                by_group(ce[h][:]), spread(a_sum[h]), -1.0 / GROUP, by_group(a[h][:]), ALU.mult, ALU.add
+            )
+
+        sq = work("sq")
+        den2 = work("den2")
+        inv = work("inv")
+        inv2 = work("inv2")
+        pp = work("pp")
+        qq = work("qq")
+        for h in halves:
+            nc.scalar.activation(out=sq[h][:], in_=ce[h][:], func=ACT.Square)
+            nc.scalar.activation(out=den2[h][:], in_=sq[h][:], func=ACT.Square, scale=sharp_sb[:], bias=1.0)
+            nc.scalar.activation(out=inv[h][:], in_=den2[h][:], func=ACT.Abs_reciprocal_sqrt)
+            nc.scalar.activation(out=inv2[h][:], in_=inv[h][:], func=ACT.Square)
+            nc.vector.scalar_tensor_tensor(pp[h][:], ce[h][:], slope[:], a[h][:], ALU.mult, ALU.mult)
+
+        def gradient_product(h):
+            dy_codes, dy_scales = quantise("dy%d" % h, dy_grouped[h], HALF)
+            nc.tensor.matmul_mx(
+                out=c0[h][:],
+                lhsT=wo_codes[:].bitcast(FP8X4),
+                lhsT_scale=wo_scales[:],
+                rhs=dy_codes[:].bitcast(FP8X4),
+                rhs_scale=dy_scales[:],
+                start=True,
+                stop=True,
+            )
+
+        interleave(nc.vector.tensor_copy, dy_grouped[1][:], dy_raw[1][:])
+        gradient_product(0)
+        gradient_product(1)
+        for h in halves:
+            nc.vector.scalar_tensor_tensor(qq[h][:], sq[h][:], sharp_sb[:], pp[h][:], ALU.mult, ALU.add)
+
+        vv = work("vv")
+        dce = work("dce")
+        tot = work("tot")
+        acc = work("acc")
+        res = work("res")
+        d_sum = sums("d_sum")
+        for h in halves:
+            nc.vector.tensor_tensor(vv[h][:], c0[h][:], inv2[h][:], ALU.mult)
+        for h in halves:
+            nc.vector.tensor_tensor(dce[h][:], vv[h][:], pp[h][:], ALU.mult)
+        for h in halves:
+            nc.vector.scalar_tensor_tensor(tot[h][:], qq[h][:], 1.0, vv[h][:], ALU.add, ALU.mult)
+        for h in halves:
+            nc.vector.tensor_reduce(d_sum[h][:], by_group(dce[h][:]), AX.X, ALU.add)
+        for h in halves:
+            nc.vector.tensor_tensor(acc[h][:], tot[h][:], old_sb[:, h * HALF : (h + 1) * HALF], ALU.add)
+        for h in halves:
+            nc.vector.scalar_tensor_tensor(
+                by_group(res[h][:]), spread(d_sum[h]), -1.0 / GROUP, by_group(acc[h][:]), ALU.mult, ALU.add
+            )
+            nc.sync.dma_start(out=out[:, h * HALF : (h + 1) * HALF], in_=res[h][:])

@@ -17,6 +17,7 @@ P = 128
 PACK = 4
 K, R, F, T, J, GROUP = 512, 128, 512, 2048, 512, 16
 HALF = J // 2
+DY_PARTS = (slice(0, 320), slice(320, J))
 FLOPS = 2 * K * R * J + 2 * F * R * J
 
 
@@ -46,30 +47,30 @@ def tile_attend_ccontrastpool_kernel(tc, tab_words, tab_scales, w1, sharp, wo, d
         word_win = tile("word_win", [P, T], U32)
         w1_raw = tile("w1_raw", [P, PACK, R], F32)
         wo_raw = tile("wo_raw", [P, PACK, R], F32)
-        dy_raw = [tile("dy_raw%d" % h, [P, PACK, HALF], F32) for h in halves]
+        dy_raw = [tile("dy_raw%d" % h, [P, PACK, c.stop - c.start], F32) for h, c in enumerate(DY_PARTS)]
         old_sb = tile("old_sb", [P, J], F32)
         sharp_sb = tile("sharp_sb", [P, 1], F32)
         warm_out = tile("warm_out", [P, 1], F32)
 
         nc.vector.memset(scale_win[:, : T // 2].bitcast(I32), 0)
         nc.gpsimd.memset(scale_win[:, T // 2 :].bitcast(I32), 0)
+        nc.sync.dma_start(out=w1_raw[:], in_=w1.rearrange("(p t) r -> p t r", t=PACK))
         nc.sync.dma_start(offsets[:], offs)
         nc.sync.dma_start(out=sharp_sb[:], in_=sharp)
-        nc.sync.dma_start(out=w1_raw[:], in_=w1.rearrange("(p t) r -> p t r", t=PACK))
         for q in range(4):
             nc.sync.dma_start(
-                out=scale_win[32 * q : 32 * q + 4, :].bitcast(I32),
-                in_=tab_scales[0, 4 * q : 4 * q + 4, :].bitcast(I32),
+                out=scale_win[q:P:32, :].bitcast(I32),
+                in_=tab_scales[0, q:16:4, :].bitcast(I32),
             )
         nc.scalar.activation(out=warm_out[:], in_=sharp_sb[:], func=ACT.Abs_reciprocal_sqrt)
         nc.sync.dma_start(
             out=word_win[:].bitcast(I32),
             in_=tab_words[0].rearrange("p n t -> p (n t)").bitcast(I32),
         )
-        nc.sync.dma_start(out=wo_raw[:], in_=wo.rearrange("(p t) r -> p t r", t=PACK))
         dy_rows = dy.rearrange("(p t) j -> p t j", t=PACK)
         for h in halves:
-            nc.sync.dma_start(out=dy_raw[h][:], in_=dy_rows[:, :, h * HALF : (h + 1) * HALF])
+            nc.sync.dma_start(out=dy_raw[h][:], in_=dy_rows[:, :, DY_PARTS[h]])
+        nc.sync.dma_start(out=wo_raw[:], in_=wo.rearrange("(p t) r -> p t r", t=PACK))
         nc.sync.dma_start(out=old_sb[:], in_=old)
 
         def quantise(name, grouped, width):
@@ -107,11 +108,11 @@ def tile_attend_ccontrastpool_kernel(tc, tab_words, tab_scales, w1, sharp, wo, d
                 stop=True,
             )
 
-        wo_grouped = tile("wo_grouped", [P, R, PACK], BF16)
-        interleave(nc.scalar.copy, wo_grouped[:], wo_raw[:])
-        dy_grouped = [tile("dy_grouped%d" % h, [P, HALF, PACK], BF16) for h in halves]
-        interleave(nc.scalar.copy, dy_grouped[0][:], dy_raw[0][:])
-        wo_codes, wo_scales = quantise("wo", wo_grouped, R)
+        dy_grouped = tile("dy_grouped", [P, J, PACK], BF16)
+        interleave(nc.scalar.copy, dy_grouped[:, DY_PARTS[0], :], dy_raw[0][:])
+        nc.gpsimd.tensor_scalar(
+            dy_grouped[:, DY_PARTS[1], :], dy_raw[1][:].rearrange("p t c -> p c t"), 1.0, 0.0, ALU.mult, ALU.add
+        )
 
         def work(name):
             return [tile("%s%d" % (name, h), [P, HALF], F32) for h in halves]
@@ -119,8 +120,8 @@ def tile_attend_ccontrastpool_kernel(tc, tab_words, tab_scales, w1, sharp, wo, d
         def sums(name):
             return [tile("%s%d" % (name, h), [P, HALF // GROUP], F32) for h in halves]
 
-        def spread(t):
-            return t[:].unsqueeze(2).to_broadcast([P, HALF // GROUP, GROUP])
+        def spread(ap):
+            return ap.unsqueeze(2).to_broadcast([P, ap.shape[1], GROUP])
 
         a_sum = sums("a_sum")
         ce = work("ce")
@@ -128,7 +129,7 @@ def tile_attend_ccontrastpool_kernel(tc, tab_words, tab_scales, w1, sharp, wo, d
             nc.vector.tensor_reduce(a_sum[h][:], by_group(a[h][:]), AX.X, ALU.add)
         for h in halves:
             nc.vector.scalar_tensor_tensor(
-                by_group(ce[h][:]), spread(a_sum[h]), -1.0 / GROUP, by_group(a[h][:]), ALU.mult, ALU.add
+                by_group(ce[h][:]), spread(a_sum[h][:]), -1.0 / GROUP, by_group(a[h][:]), ALU.mult, ALU.add
             )
 
         sq = work("sq")
@@ -139,26 +140,28 @@ def tile_attend_ccontrastpool_kernel(tc, tab_words, tab_scales, w1, sharp, wo, d
         qq = work("qq")
         for h in halves:
             nc.scalar.activation(out=sq[h][:], in_=ce[h][:], func=ACT.Square)
-            nc.scalar.activation(out=den2[h][:], in_=sq[h][:], func=ACT.Square, scale=sharp_sb[:], bias=1.0)
-            nc.scalar.activation(out=inv[h][:], in_=den2[h][:], func=ACT.Abs_reciprocal_sqrt)
-            nc.scalar.activation(out=inv2[h][:], in_=inv[h][:], func=ACT.Square)
             nc.vector.scalar_tensor_tensor(pp[h][:], ce[h][:], slope[:], a[h][:], ALU.mult, ALU.mult)
+        for h in halves:
+            nc.scalar.activation(out=den2[h][:], in_=sq[h][:], func=ACT.Square, scale=sharp_sb[:], bias=1.0)
+        for h in halves:
+            nc.scalar.activation(out=inv[h][:], in_=den2[h][:], func=ACT.Abs_reciprocal_sqrt)
+        for h in halves:
+            nc.scalar.activation(out=inv2[h][:], in_=inv[h][:], func=ACT.Square)
 
-        def gradient_product(h):
-            dy_codes, dy_scales = quantise("dy%d" % h, dy_grouped[h], HALF)
+        wo_grouped = tile("wo_grouped", [P, R, PACK], BF16)
+        interleave(nc.vector.tensor_copy, wo_grouped[:], wo_raw[:])
+        dy_codes, dy_scales = quantise("dy", dy_grouped, J)
+        wo_codes, wo_scales = quantise("wo", wo_grouped, R)
+        for h in halves:
             nc.tensor.matmul_mx(
                 out=c0[h][:],
                 lhsT=wo_codes[:].bitcast(FP8X4),
                 lhsT_scale=wo_scales[:],
-                rhs=dy_codes[:].bitcast(FP8X4),
-                rhs_scale=dy_scales[:],
+                rhs=dy_codes[:, h * HALF : (h + 1) * HALF].bitcast(FP8X4),
+                rhs_scale=dy_scales[:, h * HALF : (h + 1) * HALF],
                 start=True,
                 stop=True,
             )
-
-        interleave(nc.vector.tensor_copy, dy_grouped[1][:], dy_raw[1][:])
-        gradient_product(0)
-        gradient_product(1)
         for h in halves:
             nc.vector.scalar_tensor_tensor(qq[h][:], sq[h][:], sharp_sb[:], pp[h][:], ALU.mult, ALU.add)
 
@@ -171,15 +174,15 @@ def tile_attend_ccontrastpool_kernel(tc, tab_words, tab_scales, w1, sharp, wo, d
         for h in halves:
             nc.vector.tensor_tensor(vv[h][:], c0[h][:], inv2[h][:], ALU.mult)
         for h in halves:
-            nc.vector.tensor_tensor(dce[h][:], vv[h][:], pp[h][:], ALU.mult)
-        for h in halves:
+            nc.vector.scalar_tensor_tensor(dce[h][:], vv[h][:], -1.0 / GROUP, pp[h][:], ALU.mult, ALU.mult)
             nc.vector.scalar_tensor_tensor(tot[h][:], qq[h][:], 1.0, vv[h][:], ALU.add, ALU.mult)
-        for h in halves:
             nc.vector.tensor_reduce(d_sum[h][:], by_group(dce[h][:]), AX.X, ALU.add)
-        for h in halves:
             nc.vector.tensor_tensor(acc[h][:], tot[h][:], old_sb[:, h * HALF : (h + 1) * HALF], ALU.add)
-        for h in halves:
-            nc.vector.scalar_tensor_tensor(
-                by_group(res[h][:]), spread(d_sum[h]), -1.0 / GROUP, by_group(acc[h][:]), ALU.mult, ALU.add
+        for g in range(HALF // GROUP):
+            cols = slice(g * GROUP, (g + 1) * GROUP)
+            nc.scalar.activation(
+                out=res[0][:, cols], in_=acc[0][:, cols], func=ACT.Identity, bias=d_sum[0][:, g : g + 1]
             )
-            nc.sync.dma_start(out=out[:, h * HALF : (h + 1) * HALF], in_=res[h][:])
+        nc.scalar.dma_start(out=out[:, :HALF], in_=res[0][:])
+        nc.vector.tensor_tensor(by_group(res[1][:]), by_group(acc[1][:]), spread(d_sum[1][:]), ALU.add)
+        nc.sync.dma_start(out=out[:, HALF:], in_=res[1][:])

@@ -17,7 +17,7 @@ P = 128
 PACK = 4
 K, R, F, T, J, GROUP = 512, 128, 512, 2048, 512, 16
 HALF = J // 2
-DY_PARTS = (slice(0, 320), slice(320, J))
+DY_PARTS = (slice(0, 160), slice(160, 320), slice(320, J))
 FLOPS = 2 * K * R * J + 2 * F * R * J
 
 
@@ -56,7 +56,7 @@ def tile_attend_ccontrastpool_kernel(tc, tab_words, tab_scales, w1, sharp, wo, d
         nc.gpsimd.memset(scale_win[:, T // 2 :].bitcast(I32), 0)
         nc.sync.dma_start(out=w1_raw[:], in_=w1.rearrange("(p t) r -> p t r", t=PACK))
         nc.sync.dma_start(offsets[:], offs)
-        nc.sync.dma_start(out=sharp_sb[:], in_=sharp)
+        nc.scalar.dma_start(out=sharp_sb[:], in_=sharp)
         for q in range(4):
             nc.sync.dma_start(
                 out=scale_win[q:P:32, :].bitcast(I32),
@@ -67,10 +67,10 @@ def tile_attend_ccontrastpool_kernel(tc, tab_words, tab_scales, w1, sharp, wo, d
             out=word_win[:].bitcast(I32),
             in_=tab_words[0].rearrange("p n t -> p (n t)").bitcast(I32),
         )
-        dy_rows = dy.rearrange("(p t) j -> p t j", t=PACK)
-        for h in halves:
-            nc.sync.dma_start(out=dy_raw[h][:], in_=dy_rows[:, :, DY_PARTS[h]])
         nc.sync.dma_start(out=wo_raw[:], in_=wo.rearrange("(p t) r -> p t r", t=PACK))
+        dy_rows = dy.rearrange("(p t) j -> p t j", t=PACK)
+        for part, cols in enumerate(DY_PARTS):
+            nc.sync.dma_start(out=dy_raw[part][:], in_=dy_rows[:, :, cols])
         nc.sync.dma_start(out=old_sb[:], in_=old)
 
         def quantise(name, grouped, width):
@@ -109,10 +109,11 @@ def tile_attend_ccontrastpool_kernel(tc, tab_words, tab_scales, w1, sharp, wo, d
             )
 
         dy_grouped = tile("dy_grouped", [P, J, PACK], BF16)
-        interleave(nc.scalar.copy, dy_grouped[:, DY_PARTS[0], :], dy_raw[0][:])
-        nc.gpsimd.tensor_scalar(
-            dy_grouped[:, DY_PARTS[1], :], dy_raw[1][:].rearrange("p t c -> p c t"), 1.0, 0.0, ALU.mult, ALU.add
-        )
+        wo_grouped = tile("wo_grouped", [P, R, PACK], BF16)
+        interleave(nc.scalar.copy, wo_grouped[:], wo_raw[:])
+        for part in range(2):
+            interleave(nc.scalar.copy, dy_grouped[:, DY_PARTS[part], :], dy_raw[part][:])
+        wo_codes, wo_scales = quantise("wo", wo_grouped, R)
 
         def work(name):
             return [tile("%s%d" % (name, h), [P, HALF], F32) for h in halves]
@@ -148,11 +149,16 @@ def tile_attend_ccontrastpool_kernel(tc, tab_words, tab_scales, w1, sharp, wo, d
         for h in halves:
             nc.scalar.activation(out=inv2[h][:], in_=inv[h][:], func=ACT.Square)
 
-        wo_grouped = tile("wo_grouped", [P, R, PACK], BF16)
-        interleave(nc.vector.tensor_copy, wo_grouped[:], wo_raw[:])
-        dy_codes, dy_scales = quantise("dy", dy_grouped, J)
-        wo_codes, wo_scales = quantise("wo", wo_grouped, R)
+        interleave(nc.vector.tensor_copy, dy_grouped[:, DY_PARTS[2], :], dy_raw[2][:])
+        dy_codes = tile("dy_codes", [P, J], U32)
+        dy_scales = tile("dy_scales", [P, J], U8)
         for h in halves:
+            cols = slice(h * HALF, (h + 1) * HALF)
+            nc.vector.quantize_mx(
+                out=dy_codes[:, cols].bitcast(FP8X4),
+                scales=dy_scales[:, cols],
+                in_=dy_grouped[:, cols, :].rearrange("p c t -> p (c t)"),
+            )
             nc.tensor.matmul_mx(
                 out=c0[h][:],
                 lhsT=wo_codes[:].bitcast(FP8X4),

from contextlib import ExitStack

import concourse.mybir as mybir

F32 = mybir.dt.float32
BF16 = mybir.dt.bfloat16
I32 = mybir.dt.int32
U32 = mybir.dt.uint32
U16 = mybir.dt.uint16
U8 = mybir.dt.uint8
FP8X4 = mybir.dt.float8_e4m3fn_x4
ALU = mybir.AluOpType
ACT = mybir.ActivationFunctionType
AX = mybir.AxisListType

P = 128
PACK = 4
K, R, F, T, J, GROUP = 512, 128, 512, 2048, 512, 16
HALF = J // 2
DY_PARTS = (slice(0, 160), slice(160, 320), slice(320, J))
FLOPS = 2 * K * R * J + 2 * F * R * J


def interleave(copy, grouped, raw):
    copy(
        out=grouped.rearrange("p (c i) t -> p c t i", i=4),
        in_=raw.rearrange("p t (c i) -> p c t i", i=4),
    )


def by_group(ap):
    return ap.rearrange("p (g i) -> p g i", i=GROUP)


def tile_attend_ccontrastpool_kernel(tc, tab_words, tab_scales, w1, sharp, wo, dy, old, offs, out):
    nc = tc.nc
    halves = range(2)
    with ExitStack() as ctx:
        sb = ctx.enter_context(tc.tile_pool(name="sb", bufs=1))
        ps = ctx.enter_context(tc.psum_pool(name="ps", bufs=1))

        def tile(name, shape, dtype):
            return sb.tile(shape, dtype, name=name, align_bytes=64)

        offsets = sb.tile([P, J // 16], U16, name="offsets")
        scale_win = tile("scale_win", [P, T], U8)
        word_win = tile("word_win", [P, T], U32)
        w1_raw = tile("w1_raw", [P, PACK, R], F32)
        wo_raw = tile("wo_raw", [P, PACK, R], F32)
        dy_raw = [tile("dy_raw%d" % h, [P, PACK, c.stop - c.start], F32) for h, c in enumerate(DY_PARTS)]
        old_sb = tile("old_sb", [P, J], F32)
        sharp_sb = tile("sharp_sb", [P, 1], F32)
        warm_out = tile("warm_out", [P, 1], F32)

        nc.vector.memset(scale_win[:, : T // 2].bitcast(I32), 0)
        nc.gpsimd.memset(scale_win[:, T // 2 :].bitcast(I32), 0)
        nc.sync.dma_start(out=w1_raw[:], in_=w1.rearrange("(p t) r -> p t r", t=PACK))
        nc.sync.dma_start(offsets[:], offs)
        nc.scalar.dma_start(out=sharp_sb[:], in_=sharp)
        for q in range(4):
            nc.sync.dma_start(
                out=scale_win[q:P:32, :].bitcast(I32),
                in_=tab_scales[0, q:16:4, :].bitcast(I32),
            )
        nc.scalar.activation(out=warm_out[:], in_=sharp_sb[:], func=ACT.Abs_reciprocal_sqrt)
        nc.sync.dma_start(
            out=word_win[:].bitcast(I32),
            in_=tab_words[0].rearrange("p n t -> p (n t)").bitcast(I32),
        )
        nc.sync.dma_start(out=wo_raw[:], in_=wo.rearrange("(p t) r -> p t r", t=PACK))
        dy_rows = dy.rearrange("(p t) j -> p t j", t=PACK)
        for part, cols in enumerate(DY_PARTS):
            nc.sync.dma_start(out=dy_raw[part][:], in_=dy_rows[:, :, cols])
        nc.sync.dma_start(out=old_sb[:], in_=old)

        def quantise(name, grouped, width):
            codes = tile(name + "_codes", [P, width], U32)
            scales = tile(name + "_scales", [P, width], U8)
            nc.vector.quantize_mx(
                out=codes[:].bitcast(FP8X4),
                scales=scales[:],
                in_=grouped[:].rearrange("p c t -> p (c t)"),
            )
            return codes, scales

        w1_grouped = tile("w1_grouped", [P, R, PACK], BF16)
        interleave(nc.vector.tensor_copy, w1_grouped[:], w1_raw[:])
        tab_scale = tile("tab_scale", [P, J], U8)
        nc.vector.tensor_copy(tab_scale[:], scale_win[:].indirect(offsets[:]))
        w1_codes, w1_scales = quantise("w1", w1_grouped, R)

        slope = tile("slope", [P, 1], F32)
        nc.vector.tensor_scalar(slope[:], sharp_sb[:], -2.0, None, ALU.mult)

        a = [ps.tile([P, HALF], F32, name="a%d" % h) for h in halves]
        c0 = [ps.tile([P, HALF], F32, name="c%d" % h) for h in halves]
        for h in halves:
            tab_code = tile("tab_code%d" % h, [P, HALF], U32)
            cols = slice(h * HALF // 16, (h + 1) * HALF // 16)
            nc.vector.tensor_copy(tab_code[:], word_win[:].indirect(offsets[:, cols]))
            nc.tensor.matmul_mx(
                out=a[h][:],
                lhsT=w1_codes[:].bitcast(FP8X4),
                lhsT_scale=w1_scales[:],
                rhs=tab_code[:].bitcast(FP8X4),
                rhs_scale=tab_scale[:, h * HALF : (h + 1) * HALF],
                start=True,
                stop=True,
            )

        dy_grouped = tile("dy_grouped", [P, J, PACK], BF16)
        wo_grouped = tile("wo_grouped", [P, R, PACK], BF16)
        interleave(nc.scalar.copy, wo_grouped[:], wo_raw[:])
        for part in range(2):
            interleave(nc.scalar.copy, dy_grouped[:, DY_PARTS[part], :], dy_raw[part][:])
        wo_codes, wo_scales = quantise("wo", wo_grouped, R)

        def work(name):
            return [tile("%s%d" % (name, h), [P, HALF], F32) for h in halves]

        def sums(name):
            return [tile("%s%d" % (name, h), [P, HALF // GROUP], F32) for h in halves]

        def spread(ap):
            return ap.unsqueeze(2).to_broadcast([P, ap.shape[1], GROUP])

        a_sum = sums("a_sum")
        ce = work("ce")
        for h in halves:
            nc.vector.tensor_reduce(a_sum[h][:], by_group(a[h][:]), AX.X, ALU.add)
        for h in halves:
            nc.vector.scalar_tensor_tensor(
                by_group(ce[h][:]), spread(a_sum[h][:]), -1.0 / GROUP, by_group(a[h][:]), ALU.mult, ALU.add
            )

        sq = work("sq")
        den2 = work("den2")
        inv = work("inv")
        inv2 = work("inv2")
        pp = work("pp")
        qq = work("qq")
        for h in halves:
            nc.scalar.activation(out=sq[h][:], in_=ce[h][:], func=ACT.Square)
            nc.vector.scalar_tensor_tensor(pp[h][:], ce[h][:], slope[:], a[h][:], ALU.mult, ALU.mult)
        for h in halves:
            nc.scalar.activation(out=den2[h][:], in_=sq[h][:], func=ACT.Square, scale=sharp_sb[:], bias=1.0)
        for h in halves:
            nc.scalar.activation(out=inv[h][:], in_=den2[h][:], func=ACT.Abs_reciprocal_sqrt)
        for h in halves:
            nc.scalar.activation(out=inv2[h][:], in_=inv[h][:], func=ACT.Square)

        interleave(nc.vector.tensor_copy, dy_grouped[:, DY_PARTS[2], :], dy_raw[2][:])
        dy_codes = tile("dy_codes", [P, J], U32)
        dy_scales = tile("dy_scales", [P, J], U8)
        for h in halves:
            cols = slice(h * HALF, (h + 1) * HALF)
            nc.vector.quantize_mx(
                out=dy_codes[:, cols].bitcast(FP8X4),
                scales=dy_scales[:, cols],
                in_=dy_grouped[:, cols, :].rearrange("p c t -> p (c t)"),
            )
            nc.tensor.matmul_mx(
                out=c0[h][:],
                lhsT=wo_codes[:].bitcast(FP8X4),
                lhsT_scale=wo_scales[:],
                rhs=dy_codes[:, h * HALF : (h + 1) * HALF].bitcast(FP8X4),
                rhs_scale=dy_scales[:, h * HALF : (h + 1) * HALF],
                start=True,
                stop=True,
            )
        for h in halves:
            nc.vector.scalar_tensor_tensor(qq[h][:], sq[h][:], sharp_sb[:], pp[h][:], ALU.mult, ALU.add)

        vv = work("vv")
        dce = work("dce")
        tot = work("tot")
        acc = work("acc")
        res = work("res")
        d_sum = sums("d_sum")
        for h in halves:
            nc.vector.tensor_tensor(vv[h][:], c0[h][:], inv2[h][:], ALU.mult)
        for h in halves:
            nc.vector.scalar_tensor_tensor(dce[h][:], vv[h][:], -1.0 / GROUP, pp[h][:], ALU.mult, ALU.mult)
            nc.vector.scalar_tensor_tensor(tot[h][:], qq[h][:], 1.0, vv[h][:], ALU.add, ALU.mult)
            nc.vector.tensor_reduce(d_sum[h][:], by_group(dce[h][:]), AX.X, ALU.add)
            nc.vector.tensor_tensor(acc[h][:], tot[h][:], old_sb[:, h * HALF : (h + 1) * HALF], ALU.add)
        for g in range(HALF // GROUP):
            cols = slice(g * GROUP, (g + 1) * GROUP)
            nc.scalar.activation(
                out=res[0][:, cols], in_=acc[0][:, cols], func=ACT.Identity, bias=d_sum[0][:, g : g + 1]
            )
        nc.scalar.dma_start(out=out[:, :HALF], in_=res[0][:])
        nc.vector.tensor_tensor(by_group(res[1][:]), by_group(acc[1][:]), spread(d_sum[1][:]), ALU.add)
        nc.sync.dma_start(out=out[:, HALF:], in_=res[1][:])
